import numpy as np
import ml_dtypes


def mxq(x, axis, fmt="e4m3"):
    dtype, down = {"e4m3": (ml_dtypes.float8_e4m3fn, 7), "e5m2": (ml_dtypes.float8_e5m2, 14)}[fmt]
    v = np.moveaxis(np.asarray(x, np.float32).astype(ml_dtypes.bfloat16).astype(np.float64), axis, -1)
    blocks = v.reshape(v.shape[:-1] + (-1, 32))
    amax = np.abs(blocks).max(-1, keepdims=True)
    byte = np.maximum(np.where(amax > 0, np.frexp(amax)[1] - 1 + 127, 0) - down, 1)
    scale = np.exp2(byte - 127.0)
    codes = (blocks / scale).astype(np.float32).astype(dtype).astype(np.float64)
    return np.moveaxis((codes * scale).reshape(v.shape), -1, axis)


WIDE = False


def mx_kscale(k):
    if not WIDE:
        return np.ones(k)
    levels = np.array([10, -10, 5, -5, 0])
    if k % 512:
        return np.exp2(np.random.permutation(np.resize(levels, k // 32))).repeat(32)
    a = np.empty((k // 512, 16))
    for p in range(k // 512):
        a[p, :8] = np.random.permutation(np.resize(levels, 8))
        for g in range(8):
            far = levels[np.abs(levels - a[p, g]) >= 10]
            a[p, g + 8] = far[np.random.randint(len(far))]
    return np.exp2(a.ravel()).repeat(32)


def f64(x):
    return np.asarray(x).astype(np.float64)


def striped8(idx):
    return np.asarray(idx).reshape(8, -1, 16).transpose(0, 2, 1).reshape(128, -1).astype(np.uint16)


def unstriped8(offs):
    return offs.reshape(8, 16, -1).transpose(0, 2, 1).reshape(8, -1).astype(np.int64)


def pick8(x, idx, run):
    r = np.arange(len(x))
    return x[r[:, None], idx[r % (8 * run) // run]]


E2M1 = np.array([0.0, 0.5, 1.0, 1.5, 2.0, 3.0, 4.0, 6.0, -0.0, -0.5, -1.0, -1.5, -2.0, -3.0, -4.0, -6.0])


def pack_weight(w, fmt):
    k, n = w.shape
    w = f64(np.asarray(w, np.float32).astype(ml_dtypes.bfloat16)).reshape(k // 32, 32, n)
    amax = np.abs(w).max(1)
    if fmt == "e4m3":
        byte = np.frexp(amax)[1] - 1 + 127 - 7
    else:
        mant, ex = np.frexp(amax / 6.0)
        byte = np.where(mant > 0.5, ex, ex - 1) + 127
    byte = np.clip(np.where(amax > 0, byte, 1), 1, 254)
    scaled = (w * np.exp2(127.0 - byte)[:, None, :]).reshape(k, n).astype(np.float32)
    by_word = np.ascontiguousarray(scaled.reshape(k // 512, 128, 4, n).transpose(0, 1, 3, 2))
    if fmt == "e4m3":
        words = by_word.astype(ml_dtypes.float8_e4m3fn).view(np.uint8)
    else:
        c = by_word.astype(ml_dtypes.float4_e2m1fn).view(np.uint8) & 0xF
        words = (c[..., 0::2] | (c[..., 1::2] << 4)).reshape(k // 512, 128, 2 * n)
    return np.ascontiguousarray(words), np.ascontiguousarray(byte.astype(np.uint8).reshape(k // 512, 16, n))


def unpack_weight(words, scales, fmt):
    g, _, n = scales.shape
    words = np.ascontiguousarray(words).reshape(g, 128, n, -1)
    if fmt == "e4m3":
        vals = words.view(ml_dtypes.float8_e4m3fn).astype(np.float64)
    else:
        nib = np.empty((g, 128, n, 4), np.uint8)
        nib[..., 0::2] = words & 0xF
        nib[..., 1::2] = words >> 4
        vals = E2M1[nib]
    vals = vals * np.repeat(np.exp2(scales.astype(np.float64) - 127.0), 8, axis=1)[..., None]
    return vals.transpose(0, 1, 3, 2).reshape(g * 512, n)


def sigmoid(v):
    return 1.0 / (1.0 + np.exp(-v))


D, T, Q, I, E = 512, 1024, 128, 512, 512


def setup_inputs():
    n = np.random.standard_normal
    idx = np.stack([np.random.permutation(T)[:I] for _ in range(8)])
    fd = mx_kscale(D)
    ft = mx_kscale(T)
    keysp = pack_weight(n((D, T)) / fd[:, None], "e2m1")
    return {
        "query": (n((D, Q)) * 0.4 / np.sqrt(D) * fd[:, None]).astype(np.float32),
        "keys_words": keysp[0],
        "keys_scales": keysp[1],
        "steep": (np.random.uniform(2.0, 6.0, (Q, 1))).astype(np.float32),
        "boost": (np.random.uniform(0.5, 2.0, (1, I))).astype(np.float32),
        "fac": (np.random.uniform(8.0, 32.0, (1, T)) * ft).astype(np.float32),
        "vals": (n((T, E)) / ft[:, None]).astype(np.float32),
        "offs": striped8(idx),
    }


def reference(query, keys_words, keys_scales, steep, boost, fac, vals, offs):
    idx = unstriped8(offs)
    keysu = unpack_weight(keys_words, keys_scales, "e2m1")
    queryq = mxq(f64(query), 0, "e4m3")
    a = queryq.T @ keysu
    b = sigmoid(pick8(a, idx, 16) * f64(steep)) * f64(boost)
    bf = np.zeros((Q, T))
    bf[np.arange(Q)[:, None], idx[np.arange(Q) % 128 // 16]] = b
    s = a + bf
    p = np.exp(s - np.max(s, axis=1, keepdims=True))
    w = p * f64(fac) / np.sum(p, axis=1, keepdims=True)
    wt = w.T
    wtq = mxq(wt, 0, "e4m3")
    valsq = mxq(f64(vals), 0, "e4m3")
    o = wtq.T @ valsq
    return o

@@ -1,0 +1,241 @@
+from contextlib import ExitStack
+
+import concourse.mybir as mybir
+from concourse.masks import make_identity
+
+D, T, Q, SLOTS, E = 512, 1024, 128, 512, 512
+FLOPS = 2 * D * Q * T + 2 * T * Q * E
+
+F32 = mybir.dt.float32
+BF16 = mybir.dt.bfloat16
+I32 = mybir.dt.int32
+U32 = mybir.dt.uint32
+U16 = mybir.dt.uint16
+U8 = mybir.dt.uint8
+FP8X4 = mybir.dt.float8_e4m3fn_x4
+FP4X4 = mybir.dt.float4_e2m1fn_x4
+ACT = mybir.ActivationFunctionType
+ALU = mybir.AluOpType
+AX = mybir.AxisListType
+
+P = 128
+PACK = 4
+K_PASS = P * PACK
+HALF = 256
+
+
+def tile_attend_boost_heads_kernel(tc, query, keys_words, keys_scales, steep, boost, fac, vals, offs, out):
+    nc = tc.nc
+    with ExitStack() as ctx:
+        keep = ctx.enter_context(tc.tile_pool(name="keep", bufs=1))
+        psum = ctx.enter_context(tc.psum_pool(name="psum", bufs=1))
+
+        def sb(shape, dtype, name, tag=None):
+            return keep.tile(shape, dtype, name=name, tag=tag or name, align_bytes=64)
+
+        def bank(shape, name, tag=None):
+            return psum.tile(shape, F32, name=name, tag=tag or name)
+
+        def interleave(engine_copy, grouped, raw):
+            engine_copy(
+                out=grouped.rearrange("p (c i t) -> p c t i", i=4, t=PACK),
+                in_=raw.rearrange("p t (c i) -> p c t i", i=4),
+            )
+
+        offsets = keep.tile([P, SLOTS // 16], U16, name="offsets")
+        nc.sync.dma_start(offsets[:], offs)
+        boost_cols = sb([P, PACK], F32, "boost_cols")
+        nc.sync.dma_start(out=boost_cols[:], in_=boost.rearrange("o (p c) -> p (o c)", c=PACK))
+        q_raw = sb([P, PACK, Q], F32, "q_raw", "slot_a")
+        nc.scalar.dma_start(out=q_raw[:], in_=query.rearrange("(p j) q -> p j q", j=PACK))
+        k_words = sb([P, 2 * T], U8, "k_words")
+        nc.scalar.dma_start(out=k_words[:].bitcast(I32), in_=keys_words[0].bitcast(I32))
+
+        k_scales = sb([P, T], U8, "k_scales")
+        nc.vector.memset(k_scales[:].bitcast(I32), 0)
+        for quad in range(4):
+            nc.sync.dma_start(
+                out=k_scales[32 * quad : 32 * quad + 4, :].bitcast(I32),
+                in_=keys_scales[0, 4 * quad : 4 * quad + 4, :].bitcast(I32),
+            )
+
+        steep_col = sb([P, 1], F32, "steep_col")
+        with nc.allow_non_contiguous_dma(reason="one value a partition"):
+            nc.gpsimd.dma_start(out=steep_col[:], in_=steep)
+        ident = sb([P, P], F32, "ident")
+        make_identity(nc, ident[:])
+        fac_cols = sb([P, 2, PACK], F32, "fac_cols")
+        nc.gpsimd.dma_start(out=fac_cols[:], in_=fac.rearrange("o (g p j) -> p (o g) j", g=2, j=PACK))
+
+        zero = sb([P, 1], F32, "zero", "slot_c")
+        nc.vector.memset(zero[:], 0.0)
+        one = sb([P, 1], F32, "one")
+        nc.scalar.activation(out=one[:], in_=zero[:], func=ACT.Exp)
+        v_raw0 = sb([P, PACK, E], F32, "v_raw0", "slot_c")
+        nc.sync.dma_start(out=v_raw0[:], in_=vals[0:K_PASS, :].rearrange("(p j) e -> p j e", j=PACK))
+        raised = sb([P, T], F32, "raised")
+        nc.vector.memset(raised[:], 0.0)
+
+        q_grouped = sb([P, Q * PACK], BF16, "q_grouped", "slot_b")
+        interleave(nc.vector.tensor_copy, q_grouped[:], q_raw[:])
+        q_codes = sb([P, Q], U32, "q_codes")
+        q_scales = sb([P, Q], U8, "q_scales")
+        nc.vector.quantize_mx(out=q_codes[:].bitcast(FP8X4), scales=q_scales[:], in_=q_grouped[:])
+
+        v_raw1 = []
+        for h, tag in enumerate(("slot_a", "slot_b")):
+            raw = sb([P, PACK, HALF], F32, "v_raw1_%d" % h, tag)
+            nc.sync.dma_start(
+                out=raw[:],
+                in_=vals[K_PASS : 2 * K_PASS, HALF * h : HALF * (h + 1)].rearrange("(p j) e -> p j e", j=PACK),
+            )
+            v_raw1.append(raw)
+
+        scores = sb([P, T], F32, "scores")
+        for n in range(T // HALF):
+            cols = slice(HALF * n, HALF * (n + 1))
+            acc = bank([P, HALF], "score_bank%d" % n)
+            nc.tensor.matmul_mx(
+                out=acc[:],
+                lhsT=q_codes[:].bitcast(FP8X4),
+                lhsT_scale=q_scales[:],
+                rhs=k_words[:, 2 * HALF * n : 2 * HALF * (n + 1)].bitcast(FP4X4),
+                rhs_scale=k_scales[:, cols],
+                start=True,
+                stop=True,
+            )
+            if n % 2 == 0:
+                nc.scalar.copy(out=scores[:, cols], in_=acc[:])
+            else:
+                nc.vector.tensor_copy(out=scores[:, cols], in_=acc[:])
+
+        boost_bank = bank([P, PACK, P], "boost_bank", "score_bank0")
+        for c in range(PACK):
+            nc.tensor.transpose(boost_bank[:, c, :], boost_cols[:, c : c + 1].to_broadcast([P, P]), ident[:])
+        half_boost = sb([P, SLOTS], F32, "half_boost")
+        nc.scalar.activation(
+            out=half_boost[:].rearrange("p (n c) -> p n c", c=PACK),
+            in_=boost_bank[:].rearrange("p c n -> p n c"),
+            func=ACT.Copy,
+            scale=0.5,
+        )
+        fac_banks = []
+        for g in range(2):
+            fac_bank = bank([P, PACK, P], "fac_bank%d" % g, "score_bank%d" % (2 + g))
+            for j in range(PACK):
+                nc.tensor.transpose(fac_bank[:, j, :], fac_cols[:, g, j : j + 1].to_broadcast([P, P]), ident[:])
+            fac_banks.append(fac_bank)
+
+        picked = []
+        for c in range(2):
+            half_picked = sb([P, HALF], F32, "picked%d" % c)
+            nc.vector.tensor_scalar(
+                out=half_picked[:],
+                in0=scores[:].indirect(offsets[:, 16 * c : 16 * (c + 1)]),
+                scalar1=0.5,
+                scalar2=0.0,
+                op0=ALU.mult,
+                op1=ALU.add,
+            )
+            picked.append(half_picked)
+        pieces = ((0, 128), (128, 256), (256, 512))
+        gates = []
+        for c, (lo, hi) in enumerate(pieces):
+            bent = sb([P, hi - lo], F32, "bent%d" % c)
+            src = picked[lo // HALF][:, lo % HALF : lo % HALF + hi - lo]
+            nc.scalar.activation(out=bent[:], in_=src, func=ACT.Tanh, scale=steep_col[:])
+            gate = sb([P, hi - lo], F32, "gate%d" % c)
+            nc.scalar.activation(out=gate[:], in_=bent[:], func=ACT.Identity, bias=one[:])
+            gates.append(gate)
+        for c, (lo, hi) in enumerate(pieces):
+            nc.vector.tensor_tensor(
+                raised[:].indirect(offsets[:, lo // 16 : hi // 16]), gates[c][:], half_boost[:, lo:hi], ALU.mult
+            )
+
+        early = sb([P, 3 * HALF * PACK], BF16, "v_grouped_early", "bent2")
+        v_grouped0 = early[:, 0 : E * PACK]
+        for h in range(2):
+            interleave(
+                nc.scalar.copy,
+                early[:, HALF * PACK * h : HALF * PACK * (h + 1)],
+                v_raw0[:, :, HALF * h : HALF * (h + 1)],
+            )
+        v_grouped1 = [early[:, E * PACK : 3 * HALF * PACK]]
+        interleave(nc.scalar.copy, v_grouped1[0], v_raw1[0][:])
+
+        total = sb([P, T], F32, "total")
+        nc.vector.tensor_tensor(total[:], scores[:], raised[:], ALU.add)
+        neg_max = sb([P, 1], F32, "neg_max")
+        nc.vector.tensor_reduce(out=neg_max[:], in_=total[:], axis=AX.X, op=ALU.max, negate=True)
+        probs = sb([P, T], F32, "probs", "slot_a")
+        row_sum = sb([P, 1], F32, "row_sum")
+        nc.scalar.activation(
+            out=probs[:].rearrange("p (u m e) -> p u m e", u=2, e=2),
+            in_=total[:].rearrange("p (m u e) -> p u m e", u=2, e=2),
+            func=ACT.Exp,
+            bias=neg_max[:],
+            accum_out=row_sum[:],
+        )
+        late = sb([P, HALF * PACK], BF16, "v_grouped_late", "total")
+        v_grouped1.append(late[:])
+        interleave(nc.scalar.copy, v_grouped1[1], v_raw1[1][:])
+
+        v_codes0 = sb([P, E], U32, "v_codes0", "scores")
+        v_scales0 = sb([P, E], U8, "v_scales0")
+        nc.vector.quantize_mx(out=v_codes0[:].bitcast(FP8X4), scales=v_scales0[:], in_=v_grouped0)
+        v_codes1 = [sb([P, HALF], U32, "v_codes1_0", "raised")]
+        v_scales1 = [sb([P, HALF], U8, "v_scales1_%d" % h) for h in range(2)]
+        nc.vector.quantize_mx(out=v_codes1[0][:].bitcast(FP8X4), scales=v_scales1[0][:], in_=v_grouped1[0])
+
+        inv_sum = sb([P, 1], F32, "inv_sum")
+        nc.vector.reciprocal(out=inv_sum[:], in_=row_sum[:])
+
+        w_grouped = []
+        for g in range(2):
+            w_bank = bank([P, 2, Q], "w_bank%d" % g)
+            for u in range(2):
+                w = sb([P, HALF], BF16, "w%d%d" % (g, u))
+                first = K_PASS * u + HALF * g
+                nc.vector.scalar_tensor_tensor(
+                    out=w[:].rearrange("p (m e) -> p m e", e=2),
+                    in0=probs[:, first : first + HALF].rearrange("p (m e) -> p m e", e=2),
+                    scalar=inv_sum[:],
+                    in1=fac_banks[g][:, 2 * u : 2 * u + 2, :].rearrange("p e m -> p m e"),
+                    op0=ALU.mult,
+                    op1=ALU.mult,
+                )
+                nc.tensor.transpose(w_bank[:, u, :], w[:].bitcast(F32), ident[:])
+            grouped = sb([P, Q * PACK], BF16, "w_grouped%d" % g)
+            nc.scalar.copy(
+                out=grouped[:].bitcast(F32).rearrange("p (q u) -> p q u", u=2),
+                in_=w_bank[:].rearrange("p u q -> p q u"),
+            )
+            w_grouped.append(grouped)
+
+        out_banks = [bank([P, HALF], "out_bank%d" % h) for h in range(2)]
+        for g in range(2):
+            w_codes = sb([P, Q], U32, "w_codes%d" % g)
+            w_scales = sb([P, Q], U8, "w_scales%d" % g)
+            if g == 1:
+                v_codes1.append(sb([P, HALF], U32, "v_codes1_1", "slot_a"))
+                nc.vector.quantize_mx(out=v_codes1[1][:].bitcast(FP8X4), scales=v_scales1[1][:], in_=v_grouped1[1])
+            nc.vector.quantize_mx(out=w_codes[:].bitcast(FP8X4), scales=w_scales[:], in_=w_grouped[g][:])
+            for h in range(2):
+                cols = slice(HALF * h, HALF * (h + 1))
+                nc.tensor.matmul_mx(
+                    out=out_banks[h][:],
+                    lhsT=w_codes[:].bitcast(FP8X4),
+                    lhsT_scale=w_scales[:],
+                    rhs=(v_codes0[:, cols] if g == 0 else v_codes1[h][:]).bitcast(FP8X4),
+                    rhs_scale=v_scales0[:, cols] if g == 0 else v_scales1[h][:],
+                    start=(g == 0),
+                    stop=(g == 1),
+                )
+        for h in range(2):
+            result = sb([P, HALF], F32, "result%d" % h)
+            if h == 0:
+                nc.vector.tensor_copy(out=result[:], in_=out_banks[h][:])
+                nc.sync.dma_start(out=out[:, 0:HALF], in_=result[:])
+            else:
+                nc.scalar.copy(out=result[:], in_=out_banks[h][:])
+                nc.scalar.dma_start(out=out[:, HALF:E], in_=result[:])

@@ -1,7 +1,6 @@
 from contextlib import ExitStack
 
 import concourse.mybir as mybir
-from concourse.masks import make_identity
 
 D, T, Q, SLOTS, E = 512, 1024, 128, 512, 512
 FLOPS = 2 * D * Q * T + 2 * T * Q * E
@@ -46,50 +45,52 @@ def tile_attend_boost_heads_kernel(tc, query, keys_words, keys_scales, steep, bo
         nc.sync.dma_start(offsets[:], offs)
         boost_cols = sb([P, PACK], F32, "boost_cols")
         nc.sync.dma_start(out=boost_cols[:], in_=boost.rearrange("o (p c) -> p (o c)", c=PACK))
-        q_raw = sb([P, PACK, Q], F32, "q_raw", "slot_a")
+        q_raw = sb([P, PACK, Q], F32, "q_raw")
         nc.scalar.dma_start(out=q_raw[:], in_=query.rearrange("(p j) q -> p j q", j=PACK))
         k_words = sb([P, 2 * T], U8, "k_words")
         nc.scalar.dma_start(out=k_words[:].bitcast(I32), in_=keys_words[0].bitcast(I32))
 
         k_scales = sb([P, T], U8, "k_scales")
-        nc.vector.memset(k_scales[:].bitcast(I32), 0)
+        nc.gpsimd.memset(k_scales[:].bitcast(I32), 0)
         for quad in range(4):
             nc.sync.dma_start(
                 out=k_scales[32 * quad : 32 * quad + 4, :].bitcast(I32),
                 in_=keys_scales[0, 4 * quad : 4 * quad + 4, :].bitcast(I32),
             )
 
+
         steep_col = sb([P, 1], F32, "steep_col")
         with nc.allow_non_contiguous_dma(reason="one value a partition"):
-            nc.gpsimd.dma_start(out=steep_col[:], in_=steep)
-        ident = sb([P, P], F32, "ident")
-        make_identity(nc, ident[:])
-        fac_cols = sb([P, 2, PACK], F32, "fac_cols")
-        nc.gpsimd.dma_start(out=fac_cols[:], in_=fac.rearrange("o (g p j) -> p (o g) j", g=2, j=PACK))
-
-        zero = sb([P, 1], F32, "zero", "slot_c")
-        nc.vector.memset(zero[:], 0.0)
-        one = sb([P, 1], F32, "one")
-        nc.scalar.activation(out=one[:], in_=zero[:], func=ACT.Exp)
-        v_raw0 = sb([P, PACK, E], F32, "v_raw0", "slot_c")
+            nc.sync.dma_start(out=steep_col[:], in_=steep)
+        v_raw0 = sb([P, PACK, E], F32, "v_raw0")
         nc.sync.dma_start(out=v_raw0[:], in_=vals[0:K_PASS, :].rearrange("(p j) e -> p j e", j=PACK))
-        raised = sb([P, T], F32, "raised")
-        nc.vector.memset(raised[:], 0.0)
+        fac_cols = sb([P, 2, PACK], F32, "fac_cols")
+        nc.sync.dma_start(out=fac_cols[:], in_=fac.rearrange("o (g p j) -> p (o g) j", g=2, j=PACK))
+        v_raw1 = sb([P, PACK, E], F32, "v_raw1")
+        nc.sync.dma_start(out=v_raw1[:], in_=vals[K_PASS : 2 * K_PASS, :].rearrange("(p j) e -> p j e", j=PACK))
+        half_boost_cols = sb([P, PACK], F32, "half_boost_cols")
+        nc.scalar.activation(out=half_boost_cols[:], in_=boost_cols[:], func=ACT.Copy, scale=0.5)
 
-        q_grouped = sb([P, Q * PACK], BF16, "q_grouped", "slot_b")
+        q_grouped = sb([P, Q * PACK], BF16, "q_grouped")
         interleave(nc.vector.tensor_copy, q_grouped[:], q_raw[:])
         q_codes = sb([P, Q], U32, "q_codes")
         q_scales = sb([P, Q], U8, "q_scales")
         nc.vector.quantize_mx(out=q_codes[:].bitcast(FP8X4), scales=q_scales[:], in_=q_grouped[:])
 
-        v_raw1 = []
-        for h, tag in enumerate(("slot_a", "slot_b")):
-            raw = sb([P, PACK, HALF], F32, "v_raw1_%d" % h, tag)
-            nc.sync.dma_start(
-                out=raw[:],
-                in_=vals[K_PASS : 2 * K_PASS, HALF * h : HALF * (h + 1)].rearrange("(p j) e -> p j e", j=PACK),
-            )
-            v_raw1.append(raw)
+        ones = sb([P, 32], F32, "ones")
+        nc.vector.memset(ones[:], 1.0)
+        ident = sb([P, P], F32, "ident")
+        nc.gpsimd.memset(ident[:], 0.0)
+        ramp = sb([P, 32], F32, "ramp")
+        nc.vector.tensor_tensor_scan(out=ramp[:], data0=ones[:], data1=ones[:], initial=0.0, op0=ALU.mult, op1=ALU.add)
+        ramp_turned = sb([P, 32], F32, "ramp_turned")
+        nc.vector.transpose(out=ramp_turned[:], in_=ramp[:])
+        for quad in range(4):
+            rows = slice(32 * quad, 32 * (quad + 1))
+            nc.vector.tensor_tensor(ident[rows, rows], ramp[rows, :], ramp_turned[rows, :], ALU.is_equal)
+
+        raised = sb([P, T], F32, "raised")
+        nc.vector.memset(raised[:], 0.0)
 
         scores = sb([P, T], F32, "scores")
         for n in range(T // HALF):
@@ -104,21 +105,14 @@ def tile_attend_boost_heads_kernel(tc, query, keys_words, keys_scales, steep, bo
                 start=True,
                 stop=True,
             )
-            if n % 2 == 0:
+            if n % 2 == 1:
                 nc.scalar.copy(out=scores[:, cols], in_=acc[:])
             else:
                 nc.vector.tensor_copy(out=scores[:, cols], in_=acc[:])
 
         boost_bank = bank([P, PACK, P], "boost_bank", "score_bank0")
         for c in range(PACK):
-            nc.tensor.transpose(boost_bank[:, c, :], boost_cols[:, c : c + 1].to_broadcast([P, P]), ident[:])
-        half_boost = sb([P, SLOTS], F32, "half_boost")
-        nc.scalar.activation(
-            out=half_boost[:].rearrange("p (n c) -> p n c", c=PACK),
-            in_=boost_bank[:].rearrange("p c n -> p n c"),
-            func=ACT.Copy,
-            scale=0.5,
-        )
+            nc.tensor.transpose(boost_bank[:, c, :], half_boost_cols[:, c : c + 1].to_broadcast([P, P]), ident[:])
         fac_banks = []
         for g in range(2):
             fac_bank = bank([P, PACK, P], "fac_bank%d" % g, "score_bank%d" % (2 + g))
@@ -138,36 +132,29 @@ def tile_attend_boost_heads_kernel(tc, query, keys_words, keys_scales, steep, bo
                 op1=ALU.add,
             )
             picked.append(half_picked)
-        pieces = ((0, 128), (128, 256), (256, 512))
-        gates = []
-        for c, (lo, hi) in enumerate(pieces):
-            bent = sb([P, hi - lo], F32, "bent%d" % c)
-            src = picked[lo // HALF][:, lo % HALF : lo % HALF + hi - lo]
-            nc.scalar.activation(out=bent[:], in_=src, func=ACT.Tanh, scale=steep_col[:])
-            gate = sb([P, hi - lo], F32, "gate%d" % c)
-            nc.scalar.activation(out=gate[:], in_=bent[:], func=ACT.Identity, bias=one[:])
-            gates.append(gate)
-        for c, (lo, hi) in enumerate(pieces):
-            nc.vector.tensor_tensor(
-                raised[:].indirect(offsets[:, lo // 16 : hi // 16]), gates[c][:], half_boost[:, lo:hi], ALU.mult
+        lifts = sb([P, SLOTS], F32, "lifts")
+        for c in range(2):
+            bent = sb([P, HALF], F32, "bent%d" % c)
+            nc.scalar.activation(out=bent[:], in_=picked[c][:], func=ACT.Tanh, scale=steep_col[:])
+            nc.vector.scalar_tensor_tensor(
+                out=lifts[:, HALF * c : HALF * (c + 1)].rearrange("p (n c) -> p n c", c=PACK),
+                in0=bent[:].rearrange("p (n c) -> p n c", c=PACK),
+                scalar=1.0,
+                in1=boost_bank[:, :, 64 * c : 64 * (c + 1)].rearrange("p c n -> p n c"),
+                op0=ALU.add,
+                op1=ALU.mult,
             )
+        nc.vector.tensor_copy(raised[:].indirect(offsets[:]), lifts[:])
 
-        early = sb([P, 3 * HALF * PACK], BF16, "v_grouped_early", "bent2")
-        v_grouped0 = early[:, 0 : E * PACK]
-        for h in range(2):
-            interleave(
-                nc.scalar.copy,
-                early[:, HALF * PACK * h : HALF * PACK * (h + 1)],
-                v_raw0[:, :, HALF * h : HALF * (h + 1)],
-            )
-        v_grouped1 = [early[:, E * PACK : 3 * HALF * PACK]]
-        interleave(nc.scalar.copy, v_grouped1[0], v_raw1[0][:])
+        v_grouped = sb([P, 2 * E * PACK], BF16, "v_grouped", "picked1")
+        for g, raw in enumerate((v_raw0, v_raw1)):
+            interleave(nc.scalar.copy, v_grouped[:, E * PACK * g : E * PACK * (g + 1)], raw[:])
 
         total = sb([P, T], F32, "total")
         nc.vector.tensor_tensor(total[:], scores[:], raised[:], ALU.add)
         neg_max = sb([P, 1], F32, "neg_max")
         nc.vector.tensor_reduce(out=neg_max[:], in_=total[:], axis=AX.X, op=ALU.max, negate=True)
-        probs = sb([P, T], F32, "probs", "slot_a")
+        probs = sb([P, T], F32, "probs", "v_raw1")
         row_sum = sb([P, 1], F32, "row_sum")
         nc.scalar.activation(
             out=probs[:].rearrange("p (u m e) -> p u m e", u=2, e=2),
@@ -176,16 +163,15 @@ def tile_attend_boost_heads_kernel(tc, query, keys_words, keys_scales, steep, bo
             bias=neg_max[:],
             accum_out=row_sum[:],
         )
-        late = sb([P, HALF * PACK], BF16, "v_grouped_late", "total")
-        v_grouped1.append(late[:])
-        interleave(nc.scalar.copy, v_grouped1[1], v_raw1[1][:])
 
-        v_codes0 = sb([P, E], U32, "v_codes0", "scores")
-        v_scales0 = sb([P, E], U8, "v_scales0")
-        nc.vector.quantize_mx(out=v_codes0[:].bitcast(FP8X4), scales=v_scales0[:], in_=v_grouped0)
-        v_codes1 = [sb([P, HALF], U32, "v_codes1_0", "raised")]
-        v_scales1 = [sb([P, HALF], U8, "v_scales1_%d" % h) for h in range(2)]
-        nc.vector.quantize_mx(out=v_codes1[0][:].bitcast(FP8X4), scales=v_scales1[0][:], in_=v_grouped1[0])
+        v_codes = sb([P, 2 * E], U32, "v_codes", "scores")
+        v_scales = sb([P, 2 * E], U8, "v_scales")
+        for g in range(2):
+            nc.vector.quantize_mx(
+                out=v_codes[:, E * g : E * (g + 1)].bitcast(FP8X4),
+                scales=v_scales[:, E * g : E * (g + 1)],
+                in_=v_grouped[:, E * PACK * g : E * PACK * (g + 1)],
+            )
 
         inv_sum = sb([P, 1], F32, "inv_sum")
         nc.vector.reciprocal(out=inv_sum[:], in_=row_sum[:])
@@ -216,18 +202,15 @@ def tile_attend_boost_heads_kernel(tc, query, keys_words, keys_scales, steep, bo
         for g in range(2):
             w_codes = sb([P, Q], U32, "w_codes%d" % g)
             w_scales = sb([P, Q], U8, "w_scales%d" % g)
-            if g == 1:
-                v_codes1.append(sb([P, HALF], U32, "v_codes1_1", "slot_a"))
-                nc.vector.quantize_mx(out=v_codes1[1][:].bitcast(FP8X4), scales=v_scales1[1][:], in_=v_grouped1[1])
             nc.vector.quantize_mx(out=w_codes[:].bitcast(FP8X4), scales=w_scales[:], in_=w_grouped[g][:])
             for h in range(2):
-                cols = slice(HALF * h, HALF * (h + 1))
+                cols = slice(E * g + HALF * h, E * g + HALF * (h + 1))
                 nc.tensor.matmul_mx(
                     out=out_banks[h][:],
                     lhsT=w_codes[:].bitcast(FP8X4),
                     lhsT_scale=w_scales[:],
-                    rhs=(v_codes0[:, cols] if g == 0 else v_codes1[h][:]).bitcast(FP8X4),
-                    rhs_scale=v_scales0[:, cols] if g == 0 else v_scales1[h][:],
+                    rhs=v_codes[:, cols].bitcast(FP8X4),
+                    rhs_scale=v_scales[:, cols],
                     start=(g == 0),
                     stop=(g == 1),
                 )

@@ -21,6 +21,7 @@ P = 128
 PACK = 4
 K_PASS = P * PACK
 HALF = 256
+LEAD = 128
 
 
 def tile_attend_boost_heads_kernel(tc, query, keys_words, keys_scales, steep, boost, fac, vals, offs, out):
@@ -43,12 +44,8 @@ def tile_attend_boost_heads_kernel(tc, query, keys_words, keys_scales, steep, bo
 
         offsets = keep.tile([P, SLOTS // 16], U16, name="offsets")
         nc.sync.dma_start(offsets[:], offs)
-        boost_cols = sb([P, PACK], F32, "boost_cols")
-        nc.sync.dma_start(out=boost_cols[:], in_=boost.rearrange("o (p c) -> p (o c)", c=PACK))
         q_raw = sb([P, PACK, Q], F32, "q_raw")
         nc.scalar.dma_start(out=q_raw[:], in_=query.rearrange("(p j) q -> p j q", j=PACK))
-        k_words = sb([P, 2 * T], U8, "k_words")
-        nc.scalar.dma_start(out=k_words[:].bitcast(I32), in_=keys_words[0].bitcast(I32))
 
         k_scales = sb([P, T], U8, "k_scales")
         nc.gpsimd.memset(k_scales[:].bitcast(I32), 0)
@@ -59,6 +56,10 @@ def tile_attend_boost_heads_kernel(tc, query, keys_words, keys_scales, steep, bo
             )
 
 
+        k_words = sb([P, 2 * T], U8, "k_words")
+        nc.sync.dma_start(out=k_words[:].bitcast(I32), in_=keys_words[0].bitcast(I32))
+        boost_cols = sb([P, PACK], F32, "boost_cols")
+        nc.scalar.dma_start(out=boost_cols[:], in_=boost.rearrange("o (p c) -> p (o c)", c=PACK))
         steep_col = sb([P, 1], F32, "steep_col")
         with nc.allow_non_contiguous_dma(reason="one value a partition"):
             nc.sync.dma_start(out=steep_col[:], in_=steep)
@@ -68,11 +69,10 @@ def tile_attend_boost_heads_kernel(tc, query, keys_words, keys_scales, steep, bo
         nc.sync.dma_start(out=fac_cols[:], in_=fac.rearrange("o (g p j) -> p (o g) j", g=2, j=PACK))
         v_raw1 = sb([P, PACK, E], F32, "v_raw1")
         nc.sync.dma_start(out=v_raw1[:], in_=vals[K_PASS : 2 * K_PASS, :].rearrange("(p j) e -> p j e", j=PACK))
-        half_boost_cols = sb([P, PACK], F32, "half_boost_cols")
-        nc.scalar.activation(out=half_boost_cols[:], in_=boost_cols[:], func=ACT.Copy, scale=0.5)
 
         q_grouped = sb([P, Q * PACK], BF16, "q_grouped")
-        interleave(nc.vector.tensor_copy, q_grouped[:], q_raw[:])
+        interleave(nc.vector.tensor_copy, q_grouped[:, 0 : 80 * PACK], q_raw[:, :, 0:80])
+        interleave(nc.scalar.copy, q_grouped[:, 80 * PACK : Q * PACK], q_raw[:, :, 80:Q])
         q_codes = sb([P, Q], U32, "q_codes")
         q_scales = sb([P, Q], U8, "q_scales")
         nc.vector.quantize_mx(out=q_codes[:].bitcast(FP8X4), scales=q_scales[:], in_=q_grouped[:])
@@ -93,26 +93,27 @@ def tile_attend_boost_heads_kernel(tc, query, keys_words, keys_scales, steep, bo
         nc.vector.memset(raised[:], 0.0)
 
         scores = sb([P, T], F32, "scores")
-        for n in range(T // HALF):
-            cols = slice(HALF * n, HALF * (n + 1))
-            acc = bank([P, HALF], "score_bank%d" % n)
+        edges = (0, 256, 512, 768, 896, 1024)
+        for n in range(len(edges) - 1):
+            lo, hi = edges[n], edges[n + 1]
+            acc = bank([P, hi - lo], "score_bank%d" % n)
             nc.tensor.matmul_mx(
                 out=acc[:],
                 lhsT=q_codes[:].bitcast(FP8X4),
                 lhsT_scale=q_scales[:],
-                rhs=k_words[:, 2 * HALF * n : 2 * HALF * (n + 1)].bitcast(FP4X4),
-                rhs_scale=k_scales[:, cols],
+                rhs=k_words[:, 2 * lo : 2 * hi].bitcast(FP4X4),
+                rhs_scale=k_scales[:, lo:hi],
                 start=True,
                 stop=True,
             )
-            if n % 2 == 1:
-                nc.scalar.copy(out=scores[:, cols], in_=acc[:])
+            if n in (0, 2):
+                nc.vector.tensor_copy(out=scores[:, lo:hi], in_=acc[:])
             else:
-                nc.vector.tensor_copy(out=scores[:, cols], in_=acc[:])
+                nc.scalar.copy(out=scores[:, lo:hi], in_=acc[:])
 
         boost_bank = bank([P, PACK, P], "boost_bank", "score_bank0")
         for c in range(PACK):
-            nc.tensor.transpose(boost_bank[:, c, :], half_boost_cols[:, c : c + 1].to_broadcast([P, P]), ident[:])
+            nc.tensor.transpose(boost_bank[:, c, :], boost_cols[:, c : c + 1].to_broadcast([P, P]), ident[:])
         fac_banks = []
         for g in range(2):
             fac_bank = bank([P, PACK, P], "fac_bank%d" % g, "score_bank%d" % (2 + g))
@@ -132,21 +133,31 @@ def tile_attend_boost_heads_kernel(tc, query, keys_words, keys_scales, steep, bo
                 op1=ALU.add,
             )
             picked.append(half_picked)
-        lifts = sb([P, SLOTS], F32, "lifts")
-        for c in range(2):
-            bent = sb([P, HALF], F32, "bent%d" % c)
-            nc.scalar.activation(out=bent[:], in_=picked[c][:], func=ACT.Tanh, scale=steep_col[:])
-            nc.vector.scalar_tensor_tensor(
-                out=lifts[:, HALF * c : HALF * (c + 1)].rearrange("p (n c) -> p n c", c=PACK),
-                in0=bent[:].rearrange("p (n c) -> p n c", c=PACK),
-                scalar=1.0,
-                in1=boost_bank[:, :, 64 * c : 64 * (c + 1)].rearrange("p c n -> p n c"),
-                op0=ALU.add,
-                op1=ALU.mult,
+        def halve_boost(lo, hi):
+            row = sb([P, hi - lo], F32, "half_boost%d" % lo)
+            nc.scalar.activation(
+                out=row[:].rearrange("p (n c) -> p n c", c=PACK),
+                in_=boost_bank[:, :, lo // PACK : hi // PACK].rearrange("p c n -> p n c"),
+                func=ACT.Copy,
+                scale=0.5,
             )
-        nc.vector.tensor_copy(raised[:].indirect(offsets[:]), lifts[:])
+            return row
 
-        v_grouped = sb([P, 2 * E * PACK], BF16, "v_grouped", "picked1")
+        bent0 = sb([P, LEAD], F32, "bent0")
+        bent1 = sb([P, SLOTS - LEAD], F32, "bent1")
+        gate0 = sb([P, LEAD], F32, "gate0")
+        gate1 = sb([P, SLOTS - LEAD], F32, "gate1")
+        nc.scalar.activation(out=bent0[:], in_=picked[0][:, 0:LEAD], func=ACT.Tanh, scale=steep_col[:])
+        half0 = halve_boost(0, LEAD)
+        nc.scalar.activation(out=gate0[:], in_=bent0[:], func=ACT.Copy, bias=1.0)
+        nc.scalar.activation(out=bent1[:, 0 : HALF - LEAD], in_=picked[0][:, LEAD:HALF], func=ACT.Tanh, scale=steep_col[:])
+        nc.scalar.activation(out=bent1[:, HALF - LEAD :], in_=picked[1][:], func=ACT.Tanh, scale=steep_col[:])
+        half1 = halve_boost(LEAD, SLOTS)
+        nc.scalar.activation(out=gate1[:], in_=bent1[:], func=ACT.Copy, bias=1.0)
+        nc.vector.tensor_tensor(raised[:].indirect(offsets[:, 0 : LEAD // 16]), gate0[:], half0[:], ALU.mult)
+        nc.vector.tensor_tensor(raised[:].indirect(offsets[:, LEAD // 16 :]), gate1[:], half1[:], ALU.mult)
+
+        v_grouped = sb([P, 2 * E * PACK], BF16, "v_grouped", "bent1")
         for g, raw in enumerate((v_raw0, v_raw1)):
             interleave(nc.scalar.copy, v_grouped[:, E * PACK * g : E * PACK * (g + 1)], raw[:])
 
@@ -177,8 +188,8 @@ def tile_attend_boost_heads_kernel(tc, query, keys_words, keys_scales, steep, bo
         nc.vector.reciprocal(out=inv_sum[:], in_=row_sum[:])
 
         w_grouped = []
-        for g in range(2):
-            w_bank = bank([P, 2, Q], "w_bank%d" % g)
+        for g, tag in enumerate(("w_bank0", "score_bank4")):
+            w_bank = bank([P, 2, Q], "w_bank%d" % g, tag)
             for u in range(2):
                 w = sb([P, HALF], BF16, "w%d%d" % (g, u))
                 first = K_PASS * u + HALF * g
@@ -198,13 +209,14 @@ def tile_attend_boost_heads_kernel(tc, query, keys_words, keys_scales, steep, bo
             )
             w_grouped.append(grouped)
 
-        out_banks = [bank([P, HALF], "out_bank%d" % h) for h in range(2)]
+        parts = ((0, 256, "out_bank0"), (256, 384, "out_bank1"), (384, 512, "score_bank1"))
+        out_banks = [bank([P, hi - lo], "out_bank%d" % h, tag) for h, (lo, hi, tag) in enumerate(parts)]
         for g in range(2):
             w_codes = sb([P, Q], U32, "w_codes%d" % g)
             w_scales = sb([P, Q], U8, "w_scales%d" % g)
             nc.vector.quantize_mx(out=w_codes[:].bitcast(FP8X4), scales=w_scales[:], in_=w_grouped[g][:])
-            for h in range(2):
-                cols = slice(E * g + HALF * h, E * g + HALF * (h + 1))
+            for h, (lo, hi, tag) in enumerate(parts):
+                cols = slice(E * g + lo, E * g + hi)
                 nc.tensor.matmul_mx(
                     out=out_banks[h][:],
                     lhsT=w_codes[:].bitcast(FP8X4),
@@ -214,11 +226,11 @@ def tile_attend_boost_heads_kernel(tc, query, keys_words, keys_scales, steep, bo
                     start=(g == 0),
                     stop=(g == 1),
                 )
-        for h in range(2):
-            result = sb([P, HALF], F32, "result%d" % h)
-            if h == 0:
-                nc.vector.tensor_copy(out=result[:], in_=out_banks[h][:])
-                nc.sync.dma_start(out=out[:, 0:HALF], in_=result[:])
-            else:
+        for h, (lo, hi, tag) in enumerate(parts):
+            result = sb([P, hi - lo], F32, "result%d" % h)
+            if h == 1:
                 nc.scalar.copy(out=result[:], in_=out_banks[h][:])
-                nc.scalar.dma_start(out=out[:, HALF:E], in_=result[:])
+                nc.scalar.dma_start(out=out[:, lo:hi], in_=result[:])
+            else:
+                nc.vector.tensor_copy(out=result[:], in_=out_banks[h][:])
+                nc.sync.dma_start(out=out[:, lo:hi], in_=result[:])

from contextlib import ExitStack

import concourse.mybir as mybir

D, T, Q, SLOTS, E = 512, 1024, 128, 512, 512
FLOPS = 2 * D * Q * T + 2 * T * Q * E

F32 = mybir.dt.float32
BF16 = mybir.dt.bfloat16
I32 = mybir.dt.int32
U32 = mybir.dt.uint32
U16 = mybir.dt.uint16
U8 = mybir.dt.uint8
FP8X4 = mybir.dt.float8_e4m3fn_x4
FP4X4 = mybir.dt.float4_e2m1fn_x4
ACT = mybir.ActivationFunctionType
ALU = mybir.AluOpType
AX = mybir.AxisListType

P = 128
PACK = 4
K_PASS = P * PACK
HALF = 256
LEAD = 128


def tile_attend_boost_heads_kernel(tc, query, keys_words, keys_scales, steep, boost, fac, vals, offs, out):
    nc = tc.nc
    with ExitStack() as ctx:
        keep = ctx.enter_context(tc.tile_pool(name="keep", bufs=1))
        psum = ctx.enter_context(tc.psum_pool(name="psum", bufs=1))

        def sb(shape, dtype, name, tag=None):
            return keep.tile(shape, dtype, name=name, tag=tag or name, align_bytes=64)

        def bank(shape, name, tag=None):
            return psum.tile(shape, F32, name=name, tag=tag or name)

        def interleave(engine_copy, grouped, raw):
            engine_copy(
                out=grouped.rearrange("p (c i t) -> p c t i", i=4, t=PACK),
                in_=raw.rearrange("p t (c i) -> p c t i", i=4),
            )

        offsets = keep.tile([P, SLOTS // 16], U16, name="offsets")
        nc.sync.dma_start(offsets[:], offs)
        q_raw = sb([P, PACK, Q], F32, "q_raw")
        nc.scalar.dma_start(out=q_raw[:], in_=query.rearrange("(p j) q -> p j q", j=PACK))

        k_scales = sb([P, T], U8, "k_scales")
        nc.gpsimd.memset(k_scales[:].bitcast(I32), 0)
        for quad in range(4):
            nc.sync.dma_start(
                out=k_scales[32 * quad : 32 * quad + 4, :].bitcast(I32),
                in_=keys_scales[0, 4 * quad : 4 * quad + 4, :].bitcast(I32),
            )


        k_words = sb([P, 2 * T], U8, "k_words")
        nc.sync.dma_start(out=k_words[:].bitcast(I32), in_=keys_words[0].bitcast(I32))
        boost_cols = sb([P, PACK], F32, "boost_cols")
        nc.scalar.dma_start(out=boost_cols[:], in_=boost.rearrange("o (p c) -> p (o c)", c=PACK))
        steep_col = sb([P, 1], F32, "steep_col")
        with nc.allow_non_contiguous_dma(reason="one value a partition"):
            nc.sync.dma_start(out=steep_col[:], in_=steep)
        v_raw0 = sb([P, PACK, E], F32, "v_raw0")
        nc.sync.dma_start(out=v_raw0[:], in_=vals[0:K_PASS, :].rearrange("(p j) e -> p j e", j=PACK))
        fac_cols = sb([P, 2, PACK], F32, "fac_cols")
        nc.sync.dma_start(out=fac_cols[:], in_=fac.rearrange("o (g p j) -> p (o g) j", g=2, j=PACK))
        v_raw1 = sb([P, PACK, E], F32, "v_raw1")
        nc.sync.dma_start(out=v_raw1[:], in_=vals[K_PASS : 2 * K_PASS, :].rearrange("(p j) e -> p j e", j=PACK))

        q_grouped = sb([P, Q * PACK], BF16, "q_grouped")
        interleave(nc.vector.tensor_copy, q_grouped[:, 0 : 80 * PACK], q_raw[:, :, 0:80])
        interleave(nc.scalar.copy, q_grouped[:, 80 * PACK : Q * PACK], q_raw[:, :, 80:Q])
        q_codes = sb([P, Q], U32, "q_codes")
        q_scales = sb([P, Q], U8, "q_scales")
        nc.vector.quantize_mx(out=q_codes[:].bitcast(FP8X4), scales=q_scales[:], in_=q_grouped[:])

        ones = sb([P, 32], F32, "ones")
        nc.vector.memset(ones[:], 1.0)
        ident = sb([P, P], F32, "ident")
        nc.gpsimd.memset(ident[:], 0.0)
        ramp = sb([P, 32], F32, "ramp")
        nc.vector.tensor_tensor_scan(out=ramp[:], data0=ones[:], data1=ones[:], initial=0.0, op0=ALU.mult, op1=ALU.add)
        ramp_turned = sb([P, 32], F32, "ramp_turned")
        nc.vector.transpose(out=ramp_turned[:], in_=ramp[:])
        for quad in range(4):
            rows = slice(32 * quad, 32 * (quad + 1))
            nc.vector.tensor_tensor(ident[rows, rows], ramp[rows, :], ramp_turned[rows, :], ALU.is_equal)

        raised = sb([P, T], F32, "raised")
        nc.vector.memset(raised[:], 0.0)

        scores = sb([P, T], F32, "scores")
        edges = (0, 256, 512, 768, 896, 1024)
        for n in range(len(edges) - 1):
            lo, hi = edges[n], edges[n + 1]
            acc = bank([P, hi - lo], "score_bank%d" % n)
            nc.tensor.matmul_mx(
                out=acc[:],
                lhsT=q_codes[:].bitcast(FP8X4),
                lhsT_scale=q_scales[:],
                rhs=k_words[:, 2 * lo : 2 * hi].bitcast(FP4X4),
                rhs_scale=k_scales[:, lo:hi],
                start=True,
                stop=True,
            )
            if n in (0, 2):
                nc.vector.tensor_copy(out=scores[:, lo:hi], in_=acc[:])
            else:
                nc.scalar.copy(out=scores[:, lo:hi], in_=acc[:])

        boost_bank = bank([P, PACK, P], "boost_bank", "score_bank0")
        for c in range(PACK):
            nc.tensor.transpose(boost_bank[:, c, :], boost_cols[:, c : c + 1].to_broadcast([P, P]), ident[:])
        fac_banks = []
        for g in range(2):
            fac_bank = bank([P, PACK, P], "fac_bank%d" % g, "score_bank%d" % (2 + g))
            for j in range(PACK):
                nc.tensor.transpose(fac_bank[:, j, :], fac_cols[:, g, j : j + 1].to_broadcast([P, P]), ident[:])
            fac_banks.append(fac_bank)

        picked = []
        for c in range(2):
            half_picked = sb([P, HALF], F32, "picked%d" % c)
            nc.vector.tensor_scalar(
                out=half_picked[:],
                in0=scores[:].indirect(offsets[:, 16 * c : 16 * (c + 1)]),
                scalar1=0.5,
                scalar2=0.0,
                op0=ALU.mult,
                op1=ALU.add,
            )
            picked.append(half_picked)
        def halve_boost(lo, hi):
            row = sb([P, hi - lo], F32, "half_boost%d" % lo)
            nc.scalar.activation(
                out=row[:].rearrange("p (n c) -> p n c", c=PACK),
                in_=boost_bank[:, :, lo // PACK : hi // PACK].rearrange("p c n -> p n c"),
                func=ACT.Copy,
                scale=0.5,
            )
            return row

        bent0 = sb([P, LEAD], F32, "bent0")
        bent1 = sb([P, SLOTS - LEAD], F32, "bent1")
        gate0 = sb([P, LEAD], F32, "gate0")
        gate1 = sb([P, SLOTS - LEAD], F32, "gate1")
        nc.scalar.activation(out=bent0[:], in_=picked[0][:, 0:LEAD], func=ACT.Tanh, scale=steep_col[:])
        half0 = halve_boost(0, LEAD)
        nc.scalar.activation(out=gate0[:], in_=bent0[:], func=ACT.Copy, bias=1.0)
        nc.scalar.activation(out=bent1[:, 0 : HALF - LEAD], in_=picked[0][:, LEAD:HALF], func=ACT.Tanh, scale=steep_col[:])
        nc.scalar.activation(out=bent1[:, HALF - LEAD :], in_=picked[1][:], func=ACT.Tanh, scale=steep_col[:])
        half1 = halve_boost(LEAD, SLOTS)
        nc.scalar.activation(out=gate1[:], in_=bent1[:], func=ACT.Copy, bias=1.0)
        nc.vector.tensor_tensor(raised[:].indirect(offsets[:, 0 : LEAD // 16]), gate0[:], half0[:], ALU.mult)
        nc.vector.tensor_tensor(raised[:].indirect(offsets[:, LEAD // 16 :]), gate1[:], half1[:], ALU.mult)

        v_grouped = sb([P, 2 * E * PACK], BF16, "v_grouped", "bent1")
        for g, raw in enumerate((v_raw0, v_raw1)):
            interleave(nc.scalar.copy, v_grouped[:, E * PACK * g : E * PACK * (g + 1)], raw[:])

        total = sb([P, T], F32, "total")
        nc.vector.tensor_tensor(total[:], scores[:], raised[:], ALU.add)
        neg_max = sb([P, 1], F32, "neg_max")
        nc.vector.tensor_reduce(out=neg_max[:], in_=total[:], axis=AX.X, op=ALU.max, negate=True)
        probs = sb([P, T], F32, "probs", "v_raw1")
        row_sum = sb([P, 1], F32, "row_sum")
        nc.scalar.activation(
            out=probs[:].rearrange("p (u m e) -> p u m e", u=2, e=2),
            in_=total[:].rearrange("p (m u e) -> p u m e", u=2, e=2),
            func=ACT.Exp,
            bias=neg_max[:],
            accum_out=row_sum[:],
        )

        v_codes = sb([P, 2 * E], U32, "v_codes", "scores")
        v_scales = sb([P, 2 * E], U8, "v_scales")
        for g in range(2):
            nc.vector.quantize_mx(
                out=v_codes[:, E * g : E * (g + 1)].bitcast(FP8X4),
                scales=v_scales[:, E * g : E * (g + 1)],
                in_=v_grouped[:, E * PACK * g : E * PACK * (g + 1)],
            )

        inv_sum = sb([P, 1], F32, "inv_sum")
        nc.vector.reciprocal(out=inv_sum[:], in_=row_sum[:])

        w_grouped = []
        for g, tag in enumerate(("w_bank0", "score_bank4")):
            w_bank = bank([P, 2, Q], "w_bank%d" % g, tag)
            for u in range(2):
                w = sb([P, HALF], BF16, "w%d%d" % (g, u))
                first = K_PASS * u + HALF * g
                nc.vector.scalar_tensor_tensor(
                    out=w[:].rearrange("p (m e) -> p m e", e=2),
                    in0=probs[:, first : first + HALF].rearrange("p (m e) -> p m e", e=2),
                    scalar=inv_sum[:],
                    in1=fac_banks[g][:, 2 * u : 2 * u + 2, :].rearrange("p e m -> p m e"),
                    op0=ALU.mult,
                    op1=ALU.mult,
                )
                nc.tensor.transpose(w_bank[:, u, :], w[:].bitcast(F32), ident[:])
            grouped = sb([P, Q * PACK], BF16, "w_grouped%d" % g)
            nc.scalar.copy(
                out=grouped[:].bitcast(F32).rearrange("p (q u) -> p q u", u=2),
                in_=w_bank[:].rearrange("p u q -> p q u"),
            )
            w_grouped.append(grouped)

        parts = ((0, 256, "out_bank0"), (256, 384, "out_bank1"), (384, 512, "score_bank1"))
        out_banks = [bank([P, hi - lo], "out_bank%d" % h, tag) for h, (lo, hi, tag) in enumerate(parts)]
        for g in range(2):
            w_codes = sb([P, Q], U32, "w_codes%d" % g)
            w_scales = sb([P, Q], U8, "w_scales%d" % g)
            nc.vector.quantize_mx(out=w_codes[:].bitcast(FP8X4), scales=w_scales[:], in_=w_grouped[g][:])
            for h, (lo, hi, tag) in enumerate(parts):
                cols = slice(E * g + lo, E * g + hi)
                nc.tensor.matmul_mx(
                    out=out_banks[h][:],
                    lhsT=w_codes[:].bitcast(FP8X4),
                    lhsT_scale=w_scales[:],
                    rhs=v_codes[:, cols].bitcast(FP8X4),
                    rhs_scale=v_scales[:, cols],
                    start=(g == 0),
                    stop=(g == 1),
                )
        for h, (lo, hi, tag) in enumerate(parts):
            result = sb([P, hi - lo], F32, "result%d" % h)
            if h == 1:
                nc.scalar.copy(out=result[:], in_=out_banks[h][:])
                nc.scalar.dma_start(out=out[:, lo:hi], in_=result[:])
            else:
                nc.vector.tensor_copy(out=result[:], in_=out_banks[h][:])
                nc.sync.dma_start(out=out[:, lo:hi], in_=result[:])
